import numpy as np, ml_dtypes
CORES = [3,5,19,21,35,37,51,53,67,69]
N = 10
NP, TK = 8, 64
def setup_inputs(rng):
    return {"x": rng.standard_normal((N, 128, TK), dtype=np.float32).astype(ml_dtypes.bfloat16), "w1": (rng.standard_normal((N, 128, 128), dtype=np.float32) / 8).astype(ml_dtypes.bfloat16), "w2": (rng.standard_normal((N, 128, NP * 128), dtype=np.float32) / 8).astype(ml_dtypes.bfloat16)}
def setup_inputs_big(rng):
    d = setup_inputs(rng)
    for k in ("x", "w1", "w2"): d[k] = (d[k].astype(np.float32) * 1024.0).astype(d[k].dtype)
    return d
def setup_inputs_small(rng):
    d = setup_inputs(rng)
    for k in ("x", "w1", "w2"): d[k] = (d[k].astype(np.float32) * (1 / 1024.0)).astype(d[k].dtype)
    return d
def setup_inputs_apart(rng):
    d = setup_inputs(rng)
    f = (10.0 ** rng.permutation(np.linspace(-1.5, 1.5, N))).astype(np.float32).reshape(N, 1, 1)
    for k in ("x", "w1", "w2"): d[k] = (d[k].astype(np.float32) * f).astype(d[k].dtype)
    return d
def reference(x, w1, w2):
    X, W1, W2 = x.astype(np.float64), w1.astype(np.float64), w2.astype(np.float64)
    h = [np.maximum(W1[p].T @ X[p], 0.0) for p in range(NP)]
    y = np.full((N, 128, TK), np.nan)
    for q in range(NP, N):
        y[q] = sum(W2[q][:, 128 * p:128 * p + 128].T @ h[p] for p in range(NP))
    return {"y": y.astype(ml_dtypes.bfloat16 if x.dtype != np.float64 else np.float64)}

from concourse.bass import DstId, RemoteDMATransfer
from concourse.mybir import AluOpType

NP, TK, D = 8, 64, 128

SCRATCH = {
    "xs":   ("sbuf", [128, TK], "bfloat16"),
    "w1s":  ("sbuf", [128, D], "bfloat16"),
    "zs":   ("sbuf", [128, TK], "float32"),
    "hs":   ("sbuf", [128, TK], "bfloat16"),
    "w2s":  ("sbuf", [128, NP * D], "bfloat16"),
    "land": ("sbuf", [128, NP * TK], "bfloat16"),
    "ys":   ("sbuf", [128, TK], "bfloat16"),
    "ps":   ("psum", [128, TK], "float32"),
}
SEMAPHORES = ["ld", "z", "mm", "hr", "sent", "st"] + ["a%d" % p for p in range(NP)]


def _split(mask, parts):
    bits = [1 << b for b in range(mask.bit_length()) if (mask >> b) & 1]
    n = len(bits) // parts
    return [sum(bits[k * n:(k + 1) * n]) for k in range(parts)], n


def rank_program(g, core, T, topo):
    rank = T.rank_of(core)
    if rank is None:
        return
    S = T.sem
    qs = list(T.cores[NP:])

    if rank < NP:
        g.sync.dma_start(T.w1s[:], T.w1[:]).then_inc(S.ld, 16)
        g.scalar.dma_start(T.xs[:], T.x[:]).then_inc(S.ld, 16)
        g.vector.memset(T.zs[:], 0.0).then_inc(S.z, 1)
        g.tensor.wait_ge(S.ld, 32)
        g.tensor.matmul(T.ps[:], T.w1s[:], T.xs[:], True, True).then_inc(S.mm, 1)
        g.vector.wait_ge(S.z, 1)
        g.vector.wait_ge(S.mm, 1)
        g.vector.tensor_tensor(T.hs[:], T.ps[:], T.zs[:], AluOpType.max).then_inc(S.hr, 1)
        common = topo.mask(core, qs[0])
        for q in qs[1:]:
            common &= topo.mask(core, q)
        masks, n = _split(common, len(qs))
        slot = T.land[:, rank * TK:(rank + 1) * TK]
        trs = []
        for q, m in zip(qs, masks):
            rid, pid, _ = topo.addr(q)
            trs.append(RemoteDMATransfer(dst_ids=[DstId(rid=rid, pnc=pid)], dma_engine_mask=m,
                                         remote_sem=S["a%d" % rank], src=T.hs[:], dst=slot))
        g.wait_ge(S.hr, 1)
        g.remote_dma_fused(trs, local_sem=S.sent)
        g.wait_ge(S.sent, n * len(qs))
        return

    half = NP * D // 2
    g.sync.dma_start(T.w2s[:, :half], T.w2[:, :half]).then_inc(S.ld, 16)
    g.scalar.dma_start(T.w2s[:, half:], T.w2[:, half:]).then_inc(S.ld, 16)
    g.tensor.wait_ge(S.ld, 32)
    for p in range(NP):
        src = T.cores[p]
        common = topo.mask(src, qs[0])
        for q in qs[1:]:
            common &= topo.mask(src, q)
        _, n = _split(common, len(qs))
        g.tensor.wait_ge(S["a%d" % p], n)
        mm = g.tensor.matmul(T.ps[:], T.w2s[:, p * D:(p + 1) * D], T.land[:, p * TK:(p + 1) * TK],
                             p == 0, p == NP - 1)
    mm.then_inc(S.mm, 1)
    g.vector.wait_ge(S.mm, 1)
    g.vector.tensor_copy(T.ys[:], T.ps[:]).then_inc(S.hr, 1)
    g.sync.wait_ge(S.hr, 1)
    g.sync.dma_start(T.y[:], T.ys[:]).then_inc(S.st, 16)
    g.sync.wait_ge(S.st, 16)
